import numpy as np
import ml_dtypes


def mxq(x, axis, fmt="e4m3"):
    dtype, down = {"e4m3": (ml_dtypes.float8_e4m3fn, 7), "e5m2": (ml_dtypes.float8_e5m2, 14)}[fmt]
    v = np.moveaxis(np.asarray(x, np.float32).astype(ml_dtypes.bfloat16).astype(np.float64), axis, -1)
    blocks = v.reshape(v.shape[:-1] + (-1, 32))
    amax = np.abs(blocks).max(-1, keepdims=True)
    byte = np.maximum(np.where(amax > 0, np.frexp(amax)[1] - 1 + 127, 0) - down, 1)
    scale = np.exp2(byte - 127.0)
    codes = (blocks / scale).astype(np.float32).astype(dtype).astype(np.float64)
    return np.moveaxis((codes * scale).reshape(v.shape), -1, axis)


WIDE = False


def mx_kscale(k, group=512):
    if not WIDE:
        return np.ones(k)
    levels = np.array([10, -10, 5, -5, 0])
    if group != 512:
        return np.exp2(np.random.permutation(np.resize(levels, k // group))).repeat(group)
    if k % 512:
        return np.exp2(np.random.permutation(np.resize(levels, k // 32))).repeat(32)
    a = np.empty((k // 512, 16))
    for p in range(k // 512):
        a[p, :8] = np.random.permutation(np.resize(levels, 8))
        for g in range(8):
            far = levels[np.abs(levels - a[p, g]) >= 10]
            a[p, g + 8] = far[np.random.randint(len(far))]
    return np.exp2(a.ravel()).repeat(32)


def f64(x):
    return np.asarray(x).astype(np.float64)


H, D, N = 4, 256, 1024


def setup_inputs():
    n = np.random.standard_normal
    s = mx_kscale(D, 0)[:, None]
    S = n((H, D, 128))
    S[:, :, 127] = np.random.uniform(0.5, 1.5, (H, D))
    return {
        "q": n((H, D, N)).astype(np.float32),
        "qa": (np.random.uniform(0.5, 2.0, (D, 1)) * s).astype(np.float32),
        "S": (S / s).astype(np.float32),
        "og": n((H, N, 128)).astype(np.float32),
    }


def reference(q, qa, S, og):
    fq = (np.where(f64(q) > 0, f64(q) + 1.0, np.exp(np.minimum(f64(q), 0.0)))) * f64(qa)
    y = mxq(fq, 1, "e4m3").transpose(0, 2, 1) @ mxq(f64(S), 1, "e4m3")
    y = y / y[:, :, 127:128]
    y = y / (1.0 + np.exp(-f64(og)))
    return y

@@ -1,0 +1,184 @@
+from contextlib import ExitStack
+
+import concourse.mybir as mybir
+
+H, D, N, E = 4, 256, 1024, 128
+FLOPS = 2 * H * N * D * E
+
+F32 = mybir.dt.float32
+BF16 = mybir.dt.bfloat16
+U32 = mybir.dt.uint32
+U8 = mybir.dt.uint8
+FP8X4 = mybir.dt.float8_e4m3fn_x4
+ALU = mybir.AluOpType
+ACT = mybir.ActivationFunctionType
+
+P = 128
+PACK = 4
+ROWS = D // PACK
+W = 512
+T = W // P
+UNITS = [(pair, half) for pair in range(2) for half in range(2)]
+
+
+def tile_rows_read_elu1_norm_gate_kernel(tc, q, qa, S, og, out):
+    nc = tc.nc
+    q_rows = q.rearrange("h (p j) n -> (h p) j n", j=PACK)
+    s_rows = S.rearrange("(g c) (p j) e -> (c p) g (j e)", c=2, j=PACK)
+    qa_rows = qa.rearrange("(p j) o -> p (j o)", j=PACK)
+
+    with ExitStack() as ctx:
+        keep = ctx.enter_context(tc.tile_pool(name="keep", bufs=1))
+        psum = ctx.enter_context(tc.psum_pool(name="psum", bufs=1))
+        ctx.enter_context(tc.manual_schedule())
+
+        qa_t = keep.tile([P, PACK], F32, name="qa_t")
+        zero = keep.tile([P, 1], F32, name="zero")
+        one = keep.tile([P, 1], F32, name="one")
+        qa_abs = keep.tile([P, PACK], F32, name="qa_abs")
+        qa_sign = keep.tile([P, PACK], F32, name="qa_sign")
+        q_t = [keep.tile([P, PACK, W], F32, name="q%d" % u) for u in range(4)]
+        ex = [keep.tile([P, PACK, W], F32, name="ex%d" % u) for u in range(4)]
+        lin = [keep.tile([P, PACK, W], F32, name="lin%d" % u) for u in range(4)]
+        low = [keep.tile([P, PACK, W], F32, name="low%d" % u) for u in range(4)]
+        fq = [keep.tile([P, T, P, PACK], BF16, name="fq%d" % u, align_bytes=64) for u in range(4)]
+        fq_codes = [keep.tile([P, W], U32, name="fqc%d" % u, align_bytes=64) for u in range(4)]
+        fq_scales = [keep.tile([P, W], U8, name="fqs%d" % u, align_bytes=64) for u in range(4)]
+        s_t = keep.tile([P, 2, PACK, E], F32, name="s_t")
+        s_bf = keep.tile([P, 2, E, PACK], BF16, name="s_bf", align_bytes=64)
+        s_codes = keep.tile([P, 2 * E], U32, name="s_codes", align_bytes=64)
+        s_scales = keep.tile([P, 2 * E], U8, name="s_scales", align_bytes=64)
+        og_t = [keep.tile([P, 2, T * E], F32, name="og%d" % h) for h in range(H)]
+        gate = [keep.tile([P, 2, T * E], F32, name="gate%d" % h) for h in range(H)]
+        res = [[keep.tile([P, T, E], F32, name="res%d_%d" % (h, f)) for f in range(2)] for h in range(H)]
+        rcp = [[keep.tile([P, T], F32, name="rcp%d_%d" % (h, f)) for f in range(2)] for h in range(H)]
+        acc = [[psum.tile([P, T, E], F32, name="acc%d_%d" % (h, f)) for f in range(2)] for h in range(H)]
+
+        def load_q(u, j0, j1):
+            pair, half = UNITS[u]
+            nc.sync.dma_start(out=q_t[u][:, j0:j1, :], in_=q_rows[P * pair : P * (pair + 1), j0:j1, W * half : W * (half + 1)])
+
+        for c in range(2):
+            nc.scalar.dma_start(out=qa_t[ROWS * c : ROWS * (c + 1), :], in_=qa_rows)
+        nc.vector.memset(zero[:], 0.0)
+        nc.scalar.activation(out=one[:], in_=zero[:], func=ACT.Exp)
+        for j in range(PACK):
+            load_q(0, j, j + 1)
+        load_q(1, 0, 2)
+        load_q(1, 2, 4)
+        load_q(2, 0, 2)
+        nc.sync.dma_start(out=s_t[:].rearrange("p g j e -> p g (j e)"), in_=s_rows)
+        load_q(2, 2, 4)
+        load_q(3, 0, 4)
+        for h in range(H):
+            nc.sync.dma_start(out=og_t[h][:], in_=og[h].rearrange("(f m t) e -> m f (t e)", f=2, t=T))
+
+        def exp_act(u, j0, j1):
+            nc.scalar.activation(out=ex[u][:, j0:j1, :], in_=q_t[u][:, j0:j1, :], func=ACT.Exp)
+
+        def lin_act(u, j):
+            col = qa_abs[:, j : j + 1]
+            nc.scalar.activation(out=lin[u][:, j, :], in_=q_t[u][:, j, :], func=ACT.Identity, scale=col, bias=col)
+
+        def lin_dve(u, j):
+            nc.vector.tensor_scalar(out=lin[u][:, j, :], in0=q_t[u][:, j, :], scalar1=one[:], scalar2=qa_abs[:, j : j + 1], op0=ALU.add, op1=ALU.mult)
+
+        def low_dve(u, j):
+            nc.vector.tensor_scalar(out=low[u][:, j, :], in0=ex[u][:, j, :], scalar1=one[:], scalar2=qa_abs[:, j : j + 1], op0=ALU.min, op1=ALU.mult)
+
+        def join(u):
+            nc.vector.tensor_tensor(
+                out=fq[u][:].rearrange("p t m j -> p m j t"),
+                in0=lin[u][:].rearrange("p j (m t) -> p m j t", t=T),
+                in1=low[u][:].rearrange("p j (m t) -> p m j t", t=T),
+                op=ALU.max,
+            )
+
+        def quant(u):
+            nc.vector.quantize_mx(out=fq_codes[u][:].bitcast(FP8X4), scales=fq_scales[u][:], in_=fq[u][:].rearrange("p t m j -> p (t m j)"))
+
+        def state_cast(g):
+            nc.vector.tensor_tensor(
+                out=s_bf[:, g, :, :],
+                in0=s_t[:, g, :, :].rearrange("p j e -> p e j"),
+                in1=qa_sign[:].unsqueeze(1).to_broadcast([P, E, PACK]),
+                op=ALU.mult,
+            )
+
+        def state_quant():
+            nc.vector.quantize_mx(out=s_codes[:].bitcast(FP8X4), scales=s_scales[:], in_=s_bf[:].rearrange("p g e j -> p (g e j)"))
+
+        def products(u):
+            pair, half = UNITS[u]
+            for t in range(T):
+                for c in range(2):
+                    rows = slice(ROWS * c, ROWS * (c + 1))
+                    cols = slice(P * t, P * (t + 1))
+                    ecols = slice(E * pair, E * (pair + 1))
+                    nc.tensor.matmul_mx(
+                        out=acc[2 * pair + c][half][:, t, :],
+                        lhsT=fq_codes[u][rows, cols].bitcast(FP8X4),
+                        lhsT_scale=fq_scales[u][rows, cols],
+                        rhs=s_codes[rows, ecols].bitcast(FP8X4),
+                        rhs_scale=s_scales[rows, ecols],
+                        start=True,
+                        stop=True,
+                    )
+
+        def recip(h, f):
+            nc.vector.reciprocal(out=rcp[h][f][:], in_=acc[h][f][:, :, E - 1])
+
+        def finish(h, f):
+            for t in range(T):
+                nc.vector.scalar_tensor_tensor(
+                    out=res[h][f][:, t, :],
+                    in0=acc[h][f][:, t, :],
+                    scalar=rcp[h][f][:, t : t + 1],
+                    in1=gate[h][:, f, E * t : E * (t + 1)],
+                    op0=ALU.mult,
+                    op1=ALU.mult,
+                )
+            nc.sync.dma_start(
+                out=out[h, W * f : W * (f + 1), :].rearrange("(m t) e -> m (t e)", t=T),
+                in_=res[h][f][:].rearrange("p t e -> p (t e)"),
+            )
+
+        nc.vector.scalar_tensor_tensor(out=qa_abs[:], in0=qa_t[:], scalar=-1.0, in1=qa_t[:], op0=ALU.mult, op1=ALU.max)
+        nc.scalar.activation(out=qa_sign[:], in_=qa_t[:], func=ACT.Sign)
+
+        for j in range(PACK):
+            exp_act(0, j, j + 1)
+            lin_dve(0, j)
+            if j > 0:
+                low_dve(0, j - 1)
+        low_dve(0, PACK - 1)
+        join(0)
+        for u in range(1, 4):
+            exp_act(u, 0, 2)
+            exp_act(u, 2, 4)
+            for j in range(PACK):
+                lin_act(u, j)
+            low_dve(u, 0)
+            quant(u - 1)
+            for j in range(1, PACK):
+                low_dve(u, j)
+            if u == 2:
+                state_cast(0)
+                state_cast(1)
+            join(u)
+            if u == 2:
+                state_quant()
+                products(0)
+                products(1)
+            if u == 3:
+                products(2)
+        for h in range(H):
+            nc.scalar.activation(out=gate[h][:], in_=og_t[h][:], func=ACT.Sigmoid)
+        order = [(0, 0), (0, 1), (1, 0), (1, 1), (2, 0), (3, 0), (2, 1), (3, 1)]
+        recip(0, 0)
+        quant(3)
+        products(3)
+        for i, (h, f) in enumerate(order):
+            if i + 1 < len(order):
+                recip(*order[i + 1])
+            finish(h, f)

@@ -64,8 +64,8 @@ def tile_rows_read_elu1_norm_gate_kernel(tc, q, qa, S, og, out):
         nc.scalar.activation(out=one[:], in_=zero[:], func=ACT.Exp)
         for j in range(PACK):
             load_q(0, j, j + 1)
-        load_q(1, 0, 2)
-        load_q(1, 2, 4)
+        for j in range(PACK):
+            load_q(1, j, j + 1)
         load_q(2, 0, 2)
         nc.sync.dma_start(out=s_t[:].rearrange("p g j e -> p g (j e)"), in_=s_rows)
         load_q(2, 2, 4)
@@ -87,12 +87,14 @@ def tile_rows_read_elu1_norm_gate_kernel(tc, q, qa, S, og, out):
             nc.vector.tensor_scalar(out=low[u][:, j, :], in0=ex[u][:, j, :], scalar1=one[:], scalar2=qa_abs[:, j : j + 1], op0=ALU.min, op1=ALU.mult)
 
         def join(u):
-            nc.vector.tensor_tensor(
-                out=fq[u][:].rearrange("p t m j -> p m j t"),
-                in0=lin[u][:].rearrange("p j (m t) -> p m j t", t=T),
-                in1=low[u][:].rearrange("p j (m t) -> p m j t", t=T),
-                op=ALU.max,
-            )
+            for t0 in range(0, T, 2):
+                ts = slice(t0, t0 + 2)
+                nc.vector.tensor_tensor(
+                    out=fq[u][:, ts, :, :].rearrange("p t m j -> p m j t"),
+                    in0=lin[u][:].rearrange("p j (m t) -> p m j t", t=T)[:, :, :, ts],
+                    in1=low[u][:].rearrange("p j (m t) -> p m j t", t=T)[:, :, :, ts],
+                    op=ALU.max,
+                )
 
         def quant(u):
             nc.vector.quantize_mx(out=fq_codes[u][:].bitcast(FP8X4), scales=fq_scales[u][:], in_=fq[u][:].rearrange("p t m j -> p (t m j)"))
@@ -128,7 +130,8 @@ def tile_rows_read_elu1_norm_gate_kernel(tc, q, qa, S, og, out):
         def recip(h, f):
             nc.vector.reciprocal(out=rcp[h][f][:], in_=acc[h][f][:, :, E - 1])
 
-        def finish(h, f):
+        def finish(h, f, step):
+            rows = out[h, W * f : W * (f + 1), :].rearrange("(m t) e -> m t e", t=T)
             for t in range(T):
                 nc.vector.scalar_tensor_tensor(
                     out=res[h][f][:, t, :],
@@ -138,47 +141,51 @@ def tile_rows_read_elu1_norm_gate_kernel(tc, q, qa, S, og, out):
                     op0=ALU.mult,
                     op1=ALU.mult,
                 )
-            nc.sync.dma_start(
-                out=out[h, W * f : W * (f + 1), :].rearrange("(m t) e -> m (t e)", t=T),
-                in_=res[h][f][:].rearrange("p t e -> p (t e)"),
-            )
+                if (t + 1) % step == 0:
+                    ts = slice(t + 1 - step, t + 1)
+                    nc.sync.dma_start(out=rows[:, ts, :], in_=res[h][f][:, ts, :])
+
+        def gates(h):
+            nc.scalar.activation(out=gate[h][:], in_=og_t[h][:], func=ACT.Sigmoid)
 
         nc.vector.scalar_tensor_tensor(out=qa_abs[:], in0=qa_t[:], scalar=-1.0, in1=qa_t[:], op0=ALU.mult, op1=ALU.max)
         nc.scalar.activation(out=qa_sign[:], in_=qa_t[:], func=ACT.Sign)
 
         for j in range(PACK):
             exp_act(0, j, j + 1)
+        for j in range(PACK):
             lin_dve(0, j)
             if j > 0:
                 low_dve(0, j - 1)
         low_dve(0, PACK - 1)
         join(0)
         for u in range(1, 4):
-            exp_act(u, 0, 2)
-            exp_act(u, 2, 4)
+            step = 1 if u == 1 else 2
+            for j in range(0, PACK, step):
+                exp_act(u, j, j + step)
             for j in range(PACK):
                 lin_act(u, j)
-            low_dve(u, 0)
-            quant(u - 1)
-            for j in range(1, PACK):
-                low_dve(u, j)
             if u == 2:
                 state_cast(0)
                 state_cast(1)
-            join(u)
+            for j in range(PACK):
+                low_dve(u, j)
             if u == 2:
                 state_quant()
+            quant(u - 1)
+            if u == 2:
                 products(0)
-                products(1)
-            if u == 3:
-                products(2)
+            if u >= 2:
+                products(u - 1)
+            join(u)
         for h in range(H):
-            nc.scalar.activation(out=gate[h][:], in_=og_t[h][:], func=ACT.Sigmoid)
+            gates(h)
         order = [(0, 0), (0, 1), (1, 0), (1, 1), (2, 0), (3, 0), (2, 1), (3, 1)]
-        recip(0, 0)
+        recip(*order[0])
+        recip(*order[1])
         quant(3)
         products(3)
         for i, (h, f) in enumerate(order):
-            if i + 1 < len(order):
+            if 0 < i < len(order) - 1:
                 recip(*order[i + 1])
-            finish(h, f)
+            finish(h, f, T if i < len(order) - 1 else 2)

@@ -1,3 +1,4 @@
+import math
 from contextlib import ExitStack
 
 import concourse.mybir as mybir
@@ -9,6 +10,7 @@ F32 = mybir.dt.float32
 BF16 = mybir.dt.bfloat16
 U32 = mybir.dt.uint32
 U8 = mybir.dt.uint8
+I32 = mybir.dt.int32
 FP8X4 = mybir.dt.float8_e4m3fn_x4
 ALU = mybir.AluOpType
 ACT = mybir.ActivationFunctionType
@@ -35,12 +37,17 @@ def tile_rows_read_elu1_norm_gate_kernel(tc, q, qa, S, og, out):
         qa_t = keep.tile([P, PACK], F32, name="qa_t")
         zero = keep.tile([P, 1], F32, name="zero")
         one = keep.tile([P, 1], F32, name="one")
+        qa_man = keep.tile([P, PACK], I32, name="qa_man")
+        qa_exp = keep.tile([P, PACK], I32, name="qa_exp")
+        ln_man = keep.tile([P, PACK], F32, name="ln_man")
+        ln_exp = keep.tile([P, PACK], F32, name="ln_exp")
+        ln_qa = keep.tile([P, PACK], F32, name="ln_qa")
         qa_abs = keep.tile([P, PACK], F32, name="qa_abs")
         qa_sign = keep.tile([P, PACK], F32, name="qa_sign")
         q_t = [keep.tile([P, PACK, W], F32, name="q%d" % u) for u in range(4)]
-        ex = [keep.tile([P, PACK, W], F32, name="ex%d" % u) for u in range(4)]
+        ex = [keep.tile([P, PACK, W], BF16, name="ex%d" % u) for u in range(4)]
         lin = [keep.tile([P, PACK, W], F32, name="lin%d" % u) for u in range(4)]
-        low = [keep.tile([P, PACK, W], F32, name="low%d" % u) for u in range(4)]
+        low = [keep.tile([P, PACK, W], BF16, name="low%d" % u) for u in range(4)]
         fq = [keep.tile([P, T, P, PACK], BF16, name="fq%d" % u, align_bytes=64) for u in range(4)]
         fq_codes = [keep.tile([P, W], U32, name="fqc%d" % u, align_bytes=64) for u in range(4)]
         fq_scales = [keep.tile([P, W], U8, name="fqs%d" % u, align_bytes=64) for u in range(4)]
@@ -54,47 +61,52 @@ def tile_rows_read_elu1_norm_gate_kernel(tc, q, qa, S, og, out):
         rcp = [[keep.tile([P, T], F32, name="rcp%d_%d" % (h, f)) for f in range(2)] for h in range(H)]
         acc = [[psum.tile([P, T, E], F32, name="acc%d_%d" % (h, f)) for f in range(2)] for h in range(H)]
 
-        def load_q(u, j0, j1):
+        def load_q(u, j0, j1, cols):
             pair, half = UNITS[u]
-            nc.sync.dma_start(out=q_t[u][:, j0:j1, :], in_=q_rows[P * pair : P * (pair + 1), j0:j1, W * half : W * (half + 1)])
+            rows = q_rows[P * pair : P * (pair + 1), j0:j1, W * half : W * (half + 1)]
+            nc.sync.dma_start(out=q_t[u][:, j0:j1, cols], in_=rows[:, :, cols])
+
+        whole = slice(0, W)
+        halves = [slice(0, W // 2), slice(W // 2, W)]
 
         for c in range(2):
             nc.scalar.dma_start(out=qa_t[ROWS * c : ROWS * (c + 1), :], in_=qa_rows)
-        nc.vector.memset(zero[:], 0.0)
-        nc.scalar.activation(out=one[:], in_=zero[:], func=ACT.Exp)
+        nc.vector.memset(one[:], 1.0)
+        nc.scalar.activation(out=zero[:], in_=one[:], func=ACT.Ln)
+        for pair in range(2):
+            nc.sync.dma_start(out=s_t[:, pair, :, :].rearrange("p j e -> p (j e)"), in_=s_rows[:, pair, :])
+        for cols in halves:
+            load_q(0, 0, 2, cols)
+            load_q(0, 2, 4, cols)
         for j in range(PACK):
-            load_q(0, j, j + 1)
-        for j in range(PACK):
-            load_q(1, j, j + 1)
-        load_q(2, 0, 2)
-        nc.sync.dma_start(out=s_t[:].rearrange("p g j e -> p g (j e)"), in_=s_rows)
-        load_q(2, 2, 4)
-        load_q(3, 0, 4)
+            load_q(1, j, j + 1, whole)
+        load_q(2, 0, 2, whole)
+        load_q(2, 2, 4, whole)
+        load_q(3, 0, 4, whole)
         for h in range(H):
             nc.sync.dma_start(out=og_t[h][:], in_=og[h].rearrange("(f m t) e -> m f (t e)", f=2, t=T))
 
-        def exp_act(u, j0, j1):
-            nc.scalar.activation(out=ex[u][:, j0:j1, :], in_=q_t[u][:, j0:j1, :], func=ACT.Exp)
+        def exp_act(u, j, cols):
+            nc.scalar.activation(out=ex[u][:, j, cols], in_=q_t[u][:, j, cols], func=ACT.Exp, bias=ln_qa[:, j : j + 1])
 
-        def lin_act(u, j):
+        def lin_act(u, j, cols):
             col = qa_abs[:, j : j + 1]
-            nc.scalar.activation(out=lin[u][:, j, :], in_=q_t[u][:, j, :], func=ACT.Identity, scale=col, bias=col)
+            nc.scalar.activation(out=lin[u][:, j, cols], in_=q_t[u][:, j, cols], func=ACT.Identity, scale=col, bias=col)
 
-        def lin_dve(u, j):
-            nc.vector.tensor_scalar(out=lin[u][:, j, :], in0=q_t[u][:, j, :], scalar1=one[:], scalar2=qa_abs[:, j : j + 1], op0=ALU.add, op1=ALU.mult)
+        def lin_dve(u, j, cols):
+            nc.vector.tensor_scalar(out=lin[u][:, j, cols], in0=q_t[u][:, j, cols], scalar1=1.0, scalar2=qa_abs[:, j : j + 1], op0=ALU.add, op1=ALU.mult)
 
-        def low_dve(u, j):
-            nc.vector.tensor_scalar(out=low[u][:, j, :], in0=ex[u][:, j, :], scalar1=one[:], scalar2=qa_abs[:, j : j + 1], op0=ALU.min, op1=ALU.mult)
+        def low_dve(u, j, cols):
+            nc.vector.tensor_scalar(out=low[u][:, j, cols], in0=ex[u][:, j, cols], scalar1=qa_abs[:, j : j + 1], scalar2=None, op0=ALU.min)
 
-        def join(u):
-            for t0 in range(0, T, 2):
-                ts = slice(t0, t0 + 2)
-                nc.vector.tensor_tensor(
-                    out=fq[u][:, ts, :, :].rearrange("p t m j -> p m j t"),
-                    in0=lin[u][:].rearrange("p j (m t) -> p m j t", t=T)[:, :, :, ts],
-                    in1=low[u][:].rearrange("p j (m t) -> p m j t", t=T)[:, :, :, ts],
-                    op=ALU.max,
-                )
+        def join(u, cols):
+            ms = slice(cols.start // T, cols.stop // T)
+            nc.vector.tensor_tensor(
+                out=fq[u][:, :, ms, :].rearrange("p t m j -> p m j t"),
+                in0=lin[u][:, :, cols].rearrange("p j (m t) -> p m j t", t=T),
+                in1=low[u][:, :, cols].rearrange("p j (m t) -> p m j t", t=T),
+                op=ALU.max,
+            )
 
         def quant(u):
             nc.vector.quantize_mx(out=fq_codes[u][:].bitcast(FP8X4), scales=fq_scales[u][:], in_=fq[u][:].rearrange("p t m j -> p (t m j)"))
@@ -145,47 +157,66 @@ def tile_rows_read_elu1_norm_gate_kernel(tc, q, qa, S, og, out):
                     ts = slice(t + 1 - step, t + 1)
                     nc.sync.dma_start(out=rows[:, ts, :], in_=res[h][f][:, ts, :])
 
-        def gates(h):
-            nc.scalar.activation(out=gate[h][:], in_=og_t[h][:], func=ACT.Sigmoid)
+        def gates(h, f):
+            nc.scalar.activation(out=gate[h][:, f, :], in_=og_t[h][:, f, :], func=ACT.Sigmoid, bias=zero[:])
 
+        qa_bits = qa_t[:].bitcast(I32)
+        nc.vector.tensor_scalar(out=qa_man[:], in0=qa_bits, scalar1=0x007FFFFF, scalar2=0x3F800000, op0=ALU.bitwise_and, op1=ALU.bitwise_or)
+        nc.vector.tensor_scalar(out=qa_exp[:], in0=qa_bits, scalar1=23, scalar2=0xFF, op0=ALU.logical_shift_right, op1=ALU.bitwise_and)
         nc.vector.scalar_tensor_tensor(out=qa_abs[:], in0=qa_t[:], scalar=-1.0, in1=qa_t[:], op0=ALU.mult, op1=ALU.max)
+        nc.vector.tensor_scalar(out=ln_exp[:], in0=qa_exp[:], scalar1=-127.0, scalar2=math.log(2.0), op0=ALU.add, op1=ALU.mult)
+        nc.scalar.activation(out=ln_man[:], in_=qa_man[:].bitcast(F32), func=ACT.Ln)
         nc.scalar.activation(out=qa_sign[:], in_=qa_t[:], func=ACT.Sign)
+        nc.vector.tensor_tensor(out=ln_qa[:], in0=ln_man[:], in1=ln_exp[:], op=ALU.add)
 
+        first, second = halves
+        state_cast(0)
+        state_cast(1)
+        lin_dve(0, 0, first)
+        lin_dve(0, 1, first)
+        state_quant()
+        lin_dve(0, 2, first)
+        lin_dve(0, 3, first)
+        for cols in halves:
+            for j in range(PACK):
+                exp_act(0, j, cols)
         for j in range(PACK):
-            exp_act(0, j, j + 1)
+            low_dve(0, j, first)
+        lin_dve(0, 0, second)
+        lin_dve(0, 1, second)
+        join(0, first)
+        lin_dve(0, 2, second)
+        lin_dve(0, 3, second)
         for j in range(PACK):
-            lin_dve(0, j)
-            if j > 0:
-                low_dve(0, j - 1)
-        low_dve(0, PACK - 1)
-        join(0)
+            low_dve(0, j, second)
+        lin_dve(1, 0, whole)
+        join(0, second)
+        lin_dve(1, 1, whole)
+        on_vector = [4, 2, 1, 0]
         for u in range(1, 4):
-            step = 1 if u == 1 else 2
-            for j in range(0, PACK, step):
-                exp_act(u, j, j + step)
+            parts = halves if u == 3 else [whole]
             for j in range(PACK):
-                lin_act(u, j)
+                exp_act(u, j, whole)
+            for cols in parts:
+                for j in range(on_vector[u], PACK):
+                    lin_act(u, j, cols)
             if u == 2:
-                state_cast(0)
-                state_cast(1)
+                lin_dve(2, 0, whole)
             for j in range(PACK):
-                low_dve(u, j)
-            if u == 2:
-                state_quant()
+                low_dve(u, j, whole)
             quant(u - 1)
-            if u == 2:
-                products(0)
-            if u >= 2:
-                products(u - 1)
-            join(u)
-        for h in range(H):
-            gates(h)
-        order = [(0, 0), (0, 1), (1, 0), (1, 1), (2, 0), (3, 0), (2, 1), (3, 1)]
+            products(u - 1)
+            for cols in parts:
+                join(u, cols)
+        order = [(2 * pair + c, half) for pair, half in UNITS for c in range(2)]
+        for h, f in order:
+            gates(h, f)
         recip(*order[0])
         recip(*order[1])
+        recip(*order[2])
         quant(3)
         products(3)
         for i, (h, f) in enumerate(order):
-            if 0 < i < len(order) - 1:
+            if 2 <= i < len(order) - 1:
                 recip(*order[i + 1])
             finish(h, f, T if i < len(order) - 1 else 2)

@@ -43,7 +43,7 @@ def tile_rows_read_elu1_norm_gate_kernel(tc, q, qa, S, og, out):
         ln_exp = keep.tile([P, PACK], F32, name="ln_exp")
         ln_qa = keep.tile([P, PACK], F32, name="ln_qa")
         qa_abs = keep.tile([P, PACK], F32, name="qa_abs")
-        qa_sign = keep.tile([P, PACK], F32, name="qa_sign")
+        qa_sign = keep.tile([P, PACK], I32, name="qa_sign")
         q_t = [keep.tile([P, PACK, W], F32, name="q%d" % u) for u in range(4)]
         ex = [keep.tile([P, PACK, W], BF16, name="ex%d" % u) for u in range(4)]
         lin = [keep.tile([P, PACK, W], F32, name="lin%d" % u) for u in range(4)]
@@ -75,16 +75,15 @@ def tile_rows_read_elu1_norm_gate_kernel(tc, q, qa, S, og, out):
         nc.scalar.activation(out=zero[:], in_=one[:], func=ACT.Ln)
         for pair in range(2):
             nc.sync.dma_start(out=s_t[:, pair, :, :].rearrange("p j e -> p (j e)"), in_=s_rows[:, pair, :])
-        for cols in halves:
-            load_q(0, 0, 2, cols)
-            load_q(0, 2, 4, cols)
-        for j in range(PACK):
-            load_q(1, j, j + 1, whole)
+        for u in range(2):
+            for j in range(PACK):
+                load_q(u, j, j + 1, whole)
         load_q(2, 0, 2, whole)
         load_q(2, 2, 4, whole)
         load_q(3, 0, 4, whole)
-        for h in range(H):
-            nc.sync.dma_start(out=og_t[h][:], in_=og[h].rearrange("(f m t) e -> m f (t e)", f=2, t=T))
+        for u, (pair, half) in enumerate(UNITS):
+            rows = og[2 * pair : 2 * pair + 2, W * half : W * (half + 1), :]
+            nc.sync.dma_start(out=og_t[u][:], in_=rows.rearrange("c (m t) e -> m c (t e)", t=T))
 
         def exp_act(u, j, cols):
             nc.scalar.activation(out=ex[u][:, j, cols], in_=q_t[u][:, j, cols], func=ACT.Exp, bias=ln_qa[:, j : j + 1])
@@ -115,7 +114,7 @@ def tile_rows_read_elu1_norm_gate_kernel(tc, q, qa, S, og, out):
             nc.vector.tensor_tensor(
                 out=s_bf[:, g, :, :],
                 in0=s_t[:, g, :, :].rearrange("p j e -> p e j"),
-                in1=qa_sign[:].unsqueeze(1).to_broadcast([P, E, PACK]),
+                in1=qa_sign[:].bitcast(F32).unsqueeze(1).to_broadcast([P, E, PACK]),
                 op=ALU.mult,
             )
 
@@ -149,7 +148,7 @@ def tile_rows_read_elu1_norm_gate_kernel(tc, q, qa, S, og, out):
                     out=res[h][f][:, t, :],
                     in0=acc[h][f][:, t, :],
                     scalar=rcp[h][f][:, t : t + 1],
-                    in1=gate[h][:, f, E * t : E * (t + 1)],
+                    in1=gate[2 * (h // 2) + f][:, h % 2, E * t : E * (t + 1)],
                     op0=ALU.mult,
                     op1=ALU.mult,
                 )
@@ -157,66 +156,55 @@ def tile_rows_read_elu1_norm_gate_kernel(tc, q, qa, S, og, out):
                     ts = slice(t + 1 - step, t + 1)
                     nc.sync.dma_start(out=rows[:, ts, :], in_=res[h][f][:, ts, :])
 
-        def gates(h, f):
-            nc.scalar.activation(out=gate[h][:, f, :], in_=og_t[h][:, f, :], func=ACT.Sigmoid, bias=zero[:])
+        def gates(u):
+            nc.scalar.activation(out=gate[u][:], in_=og_t[u][:], func=ACT.Sigmoid, bias=zero[:])
 
         qa_bits = qa_t[:].bitcast(I32)
         nc.vector.tensor_scalar(out=qa_man[:], in0=qa_bits, scalar1=0x007FFFFF, scalar2=0x3F800000, op0=ALU.bitwise_and, op1=ALU.bitwise_or)
         nc.vector.tensor_scalar(out=qa_exp[:], in0=qa_bits, scalar1=23, scalar2=0xFF, op0=ALU.logical_shift_right, op1=ALU.bitwise_and)
+        nc.vector.tensor_scalar(out=qa_sign[:], in0=qa_bits, scalar1=-(1 << 31), scalar2=0x3F800000, op0=ALU.bitwise_and, op1=ALU.bitwise_or)
         nc.vector.scalar_tensor_tensor(out=qa_abs[:], in0=qa_t[:], scalar=-1.0, in1=qa_t[:], op0=ALU.mult, op1=ALU.max)
         nc.vector.tensor_scalar(out=ln_exp[:], in0=qa_exp[:], scalar1=-127.0, scalar2=math.log(2.0), op0=ALU.add, op1=ALU.mult)
         nc.scalar.activation(out=ln_man[:], in_=qa_man[:].bitcast(F32), func=ACT.Ln)
-        nc.scalar.activation(out=qa_sign[:], in_=qa_t[:], func=ACT.Sign)
         nc.vector.tensor_tensor(out=ln_qa[:], in0=ln_man[:], in1=ln_exp[:], op=ALU.add)
 
-        first, second = halves
+        def lows(u):
+            for j in reversed(range(PACK)):
+                low_dve(u, j, whole)
+
         state_cast(0)
         state_cast(1)
-        lin_dve(0, 0, first)
-        lin_dve(0, 1, first)
+        lin_dve(0, 0, whole)
+        lin_dve(0, 1, whole)
         state_quant()
-        lin_dve(0, 2, first)
-        lin_dve(0, 3, first)
-        for cols in halves:
-            for j in range(PACK):
-                exp_act(0, j, cols)
-        for j in range(PACK):
-            low_dve(0, j, first)
-        lin_dve(0, 0, second)
-        lin_dve(0, 1, second)
-        join(0, first)
-        lin_dve(0, 2, second)
-        lin_dve(0, 3, second)
-        for j in range(PACK):
-            low_dve(0, j, second)
+        lin_dve(0, 2, whole)
+        lin_dve(0, 3, whole)
         lin_dve(1, 0, whole)
-        join(0, second)
-        lin_dve(1, 1, whole)
-        on_vector = [4, 2, 1, 0]
-        for u in range(1, 4):
+        on_vector = [4, 2, 0, 0]
+        for u in range(4):
             parts = halves if u == 3 else [whole]
             for j in range(PACK):
                 exp_act(u, j, whole)
             for cols in parts:
                 for j in range(on_vector[u], PACK):
                     lin_act(u, j, cols)
-            if u == 2:
-                lin_dve(2, 0, whole)
-            for j in range(PACK):
-                low_dve(u, j, whole)
-            quant(u - 1)
-            products(u - 1)
+            lows(u)
+            if u == 0:
+                lin_dve(1, 1, whole)
+            else:
+                quant(u - 1)
+                products(u - 1)
             for cols in parts:
                 join(u, cols)
         order = [(2 * pair + c, half) for pair, half in UNITS for c in range(2)]
-        for h, f in order:
-            gates(h, f)
-        recip(*order[0])
-        recip(*order[1])
-        recip(*order[2])
+        for u in range(4):
+            gates(u)
+        for h, f in reversed(order[:6]):
+            recip(h, f)
         quant(3)
         products(3)
         for i, (h, f) in enumerate(order):
-            if 2 <= i < len(order) - 1:
-                recip(*order[i + 1])
+            if i == 5:
+                recip(*order[7])
+                recip(*order[6])
             finish(h, f, T if i < len(order) - 1 else 2)

import math
from contextlib import ExitStack

import concourse.mybir as mybir

H, D, N, E = 4, 256, 1024, 128
FLOPS = 2 * H * N * D * E

F32 = mybir.dt.float32
BF16 = mybir.dt.bfloat16
U32 = mybir.dt.uint32
U8 = mybir.dt.uint8
I32 = mybir.dt.int32
FP8X4 = mybir.dt.float8_e4m3fn_x4
ALU = mybir.AluOpType
ACT = mybir.ActivationFunctionType

P = 128
PACK = 4
ROWS = D // PACK
W = 512
T = W // P
UNITS = [(pair, half) for pair in range(2) for half in range(2)]


def tile_rows_read_elu1_norm_gate_kernel(tc, q, qa, S, og, out):
    nc = tc.nc
    q_rows = q.rearrange("h (p j) n -> (h p) j n", j=PACK)
    s_rows = S.rearrange("(g c) (p j) e -> (c p) g (j e)", c=2, j=PACK)
    qa_rows = qa.rearrange("(p j) o -> p (j o)", j=PACK)

    with ExitStack() as ctx:
        keep = ctx.enter_context(tc.tile_pool(name="keep", bufs=1))
        psum = ctx.enter_context(tc.psum_pool(name="psum", bufs=1))
        ctx.enter_context(tc.manual_schedule())

        qa_t = keep.tile([P, PACK], F32, name="qa_t")
        zero = keep.tile([P, 1], F32, name="zero")
        one = keep.tile([P, 1], F32, name="one")
        qa_man = keep.tile([P, PACK], I32, name="qa_man")
        qa_exp = keep.tile([P, PACK], I32, name="qa_exp")
        ln_man = keep.tile([P, PACK], F32, name="ln_man")
        ln_exp = keep.tile([P, PACK], F32, name="ln_exp")
        ln_qa = keep.tile([P, PACK], F32, name="ln_qa")
        qa_abs = keep.tile([P, PACK], F32, name="qa_abs")
        qa_sign = keep.tile([P, PACK], I32, name="qa_sign")
        q_t = [keep.tile([P, PACK, W], F32, name="q%d" % u) for u in range(4)]
        ex = [keep.tile([P, PACK, W], BF16, name="ex%d" % u) for u in range(4)]
        lin = [keep.tile([P, PACK, W], F32, name="lin%d" % u) for u in range(4)]
        low = [keep.tile([P, PACK, W], BF16, name="low%d" % u) for u in range(4)]
        fq = [keep.tile([P, T, P, PACK], BF16, name="fq%d" % u, align_bytes=64) for u in range(4)]
        fq_codes = [keep.tile([P, W], U32, name="fqc%d" % u, align_bytes=64) for u in range(4)]
        fq_scales = [keep.tile([P, W], U8, name="fqs%d" % u, align_bytes=64) for u in range(4)]
        s_t = keep.tile([P, 2, PACK, E], F32, name="s_t")
        s_bf = keep.tile([P, 2, E, PACK], BF16, name="s_bf", align_bytes=64)
        s_codes = keep.tile([P, 2 * E], U32, name="s_codes", align_bytes=64)
        s_scales = keep.tile([P, 2 * E], U8, name="s_scales", align_bytes=64)
        og_t = [keep.tile([P, 2, T * E], F32, name="og%d" % h) for h in range(H)]
        gate = [keep.tile([P, 2, T * E], F32, name="gate%d" % h) for h in range(H)]
        res = [[keep.tile([P, T, E], F32, name="res%d_%d" % (h, f)) for f in range(2)] for h in range(H)]
        rcp = [[keep.tile([P, T], F32, name="rcp%d_%d" % (h, f)) for f in range(2)] for h in range(H)]
        acc = [[psum.tile([P, T, E], F32, name="acc%d_%d" % (h, f)) for f in range(2)] for h in range(H)]

        def load_q(u, j0, j1, cols):
            pair, half = UNITS[u]
            rows = q_rows[P * pair : P * (pair + 1), j0:j1, W * half : W * (half + 1)]
            nc.sync.dma_start(out=q_t[u][:, j0:j1, cols], in_=rows[:, :, cols])

        whole = slice(0, W)
        halves = [slice(0, W // 2), slice(W // 2, W)]

        for c in range(2):
            nc.scalar.dma_start(out=qa_t[ROWS * c : ROWS * (c + 1), :], in_=qa_rows)
        nc.vector.memset(one[:], 1.0)
        nc.scalar.activation(out=zero[:], in_=one[:], func=ACT.Ln)
        for pair in range(2):
            nc.sync.dma_start(out=s_t[:, pair, :, :].rearrange("p j e -> p (j e)"), in_=s_rows[:, pair, :])
        for u in range(2):
            for j in range(PACK):
                load_q(u, j, j + 1, whole)
        load_q(2, 0, 2, whole)
        load_q(2, 2, 4, whole)
        load_q(3, 0, 4, whole)
        for u, (pair, half) in enumerate(UNITS):
            rows = og[2 * pair : 2 * pair + 2, W * half : W * (half + 1), :]
            nc.sync.dma_start(out=og_t[u][:], in_=rows.rearrange("c (m t) e -> m c (t e)", t=T))

        def exp_act(u, j, cols):
            nc.scalar.activation(out=ex[u][:, j, cols], in_=q_t[u][:, j, cols], func=ACT.Exp, bias=ln_qa[:, j : j + 1])

        def lin_act(u, j, cols):
            col = qa_abs[:, j : j + 1]
            nc.scalar.activation(out=lin[u][:, j, cols], in_=q_t[u][:, j, cols], func=ACT.Identity, scale=col, bias=col)

        def lin_dve(u, j, cols):
            nc.vector.tensor_scalar(out=lin[u][:, j, cols], in0=q_t[u][:, j, cols], scalar1=1.0, scalar2=qa_abs[:, j : j + 1], op0=ALU.add, op1=ALU.mult)

        def low_dve(u, j, cols):
            nc.vector.tensor_scalar(out=low[u][:, j, cols], in0=ex[u][:, j, cols], scalar1=qa_abs[:, j : j + 1], scalar2=None, op0=ALU.min)

        def join(u, cols):
            ms = slice(cols.start // T, cols.stop // T)
            nc.vector.tensor_tensor(
                out=fq[u][:, :, ms, :].rearrange("p t m j -> p m j t"),
                in0=lin[u][:, :, cols].rearrange("p j (m t) -> p m j t", t=T),
                in1=low[u][:, :, cols].rearrange("p j (m t) -> p m j t", t=T),
                op=ALU.max,
            )

        def quant(u):
            nc.vector.quantize_mx(out=fq_codes[u][:].bitcast(FP8X4), scales=fq_scales[u][:], in_=fq[u][:].rearrange("p t m j -> p (t m j)"))

        def state_cast(g):
            nc.vector.tensor_tensor(
                out=s_bf[:, g, :, :],
                in0=s_t[:, g, :, :].rearrange("p j e -> p e j"),
                in1=qa_sign[:].bitcast(F32).unsqueeze(1).to_broadcast([P, E, PACK]),
                op=ALU.mult,
            )

        def state_quant():
            nc.vector.quantize_mx(out=s_codes[:].bitcast(FP8X4), scales=s_scales[:], in_=s_bf[:].rearrange("p g e j -> p (g e j)"))

        def products(u):
            pair, half = UNITS[u]
            for t in range(T):
                for c in range(2):
                    rows = slice(ROWS * c, ROWS * (c + 1))
                    cols = slice(P * t, P * (t + 1))
                    ecols = slice(E * pair, E * (pair + 1))
                    nc.tensor.matmul_mx(
                        out=acc[2 * pair + c][half][:, t, :],
                        lhsT=fq_codes[u][rows, cols].bitcast(FP8X4),
                        lhsT_scale=fq_scales[u][rows, cols],
                        rhs=s_codes[rows, ecols].bitcast(FP8X4),
                        rhs_scale=s_scales[rows, ecols],
                        start=True,
                        stop=True,
                    )

        def recip(h, f):
            nc.vector.reciprocal(out=rcp[h][f][:], in_=acc[h][f][:, :, E - 1])

        def finish(h, f, step):
            rows = out[h, W * f : W * (f + 1), :].rearrange("(m t) e -> m t e", t=T)
            for t in range(T):
                nc.vector.scalar_tensor_tensor(
                    out=res[h][f][:, t, :],
                    in0=acc[h][f][:, t, :],
                    scalar=rcp[h][f][:, t : t + 1],
                    in1=gate[2 * (h // 2) + f][:, h % 2, E * t : E * (t + 1)],
                    op0=ALU.mult,
                    op1=ALU.mult,
                )
                if (t + 1) % step == 0:
                    ts = slice(t + 1 - step, t + 1)
                    nc.sync.dma_start(out=rows[:, ts, :], in_=res[h][f][:, ts, :])

        def gates(u):
            nc.scalar.activation(out=gate[u][:], in_=og_t[u][:], func=ACT.Sigmoid, bias=zero[:])

        qa_bits = qa_t[:].bitcast(I32)
        nc.vector.tensor_scalar(out=qa_man[:], in0=qa_bits, scalar1=0x007FFFFF, scalar2=0x3F800000, op0=ALU.bitwise_and, op1=ALU.bitwise_or)
        nc.vector.tensor_scalar(out=qa_exp[:], in0=qa_bits, scalar1=23, scalar2=0xFF, op0=ALU.logical_shift_right, op1=ALU.bitwise_and)
        nc.vector.tensor_scalar(out=qa_sign[:], in0=qa_bits, scalar1=-(1 << 31), scalar2=0x3F800000, op0=ALU.bitwise_and, op1=ALU.bitwise_or)
        nc.vector.scalar_tensor_tensor(out=qa_abs[:], in0=qa_t[:], scalar=-1.0, in1=qa_t[:], op0=ALU.mult, op1=ALU.max)
        nc.vector.tensor_scalar(out=ln_exp[:], in0=qa_exp[:], scalar1=-127.0, scalar2=math.log(2.0), op0=ALU.add, op1=ALU.mult)
        nc.scalar.activation(out=ln_man[:], in_=qa_man[:].bitcast(F32), func=ACT.Ln)
        nc.vector.tensor_tensor(out=ln_qa[:], in0=ln_man[:], in1=ln_exp[:], op=ALU.add)

        def lows(u):
            for j in reversed(range(PACK)):
                low_dve(u, j, whole)

        state_cast(0)
        state_cast(1)
        lin_dve(0, 0, whole)
        lin_dve(0, 1, whole)
        state_quant()
        lin_dve(0, 2, whole)
        lin_dve(0, 3, whole)
        lin_dve(1, 0, whole)
        on_vector = [4, 2, 0, 0]
        for u in range(4):
            parts = halves if u == 3 else [whole]
            for j in range(PACK):
                exp_act(u, j, whole)
            for cols in parts:
                for j in range(on_vector[u], PACK):
                    lin_act(u, j, cols)
            lows(u)
            if u == 0:
                lin_dve(1, 1, whole)
            else:
                quant(u - 1)
                products(u - 1)
            for cols in parts:
                join(u, cols)
        order = [(2 * pair + c, half) for pair, half in UNITS for c in range(2)]
        for u in range(4):
            gates(u)
        for h, f in reversed(order[:6]):
            recip(h, f)
        quant(3)
        products(3)
        for i, (h, f) in enumerate(order):
            if i == 5:
                recip(*order[7])
                recip(*order[6])
            finish(h, f, T if i < len(order) - 1 else 2)
